import numpy as np, ml_dtypes
CORES = [31,71,111]
N = 3
import mx_ref
NC, WT = 128, 2
LR = np.float32(2.0 ** -2)
BF = ml_dtypes.bfloat16
def cut(t, i, w=512):
    return t[:, w * i:w * i + w]
def tile(rs):
    return np.stack(rs, axis=2).reshape(128, -1).astype(BF)
def pick(b):
    s = np.zeros((128, 128, 4), np.float32)
    s[np.arange(128), np.arange(128), b] = 1.0
    return mx_ref.quantize(s.reshape(128, 512).astype(BF))
def pk(c, s, i=0):
    return (np.ascontiguousarray(c[:, 512 * i:512 * i + 512]), mx_ref.live(s[:, 128 * i:128 * i + 128]))
def inputs(rng, e, E):
    def f(*shape):
        v = (rng.standard_normal(shape, dtype=np.float32) * np.exp2(rng.integers(-2, 3, shape[:-1] + (1,)))).astype(BF)
        return mx_ref.spread((v.astype(np.float32) * np.exp2(rng.integers(-E, E + 1, shape[:-2] + (1, 1))).astype(np.float32)).astype(BF), rng, e)
    def packed(k):
        c = np.zeros((N, 128, k * 512), np.uint8); s = np.zeros((N, 128, k * 128), np.uint8)
        for r in range(N):
            for i in range(k):
                a, b = mx_ref.quantize(f(128, 512)); c[r][:, 512 * i:512 * i + 512] = a; s[r][:, 128 * i:128 * i + 128] = mx_ref.plane(b, rng)
        return c, s
    d = {}
    d["wc"], d["ws"] = packed(WT)
    d["gr"] = f(N, 128, WT * 512)
    d["x"] = f(N, 128, 4 * NC)
    return d
def setup_inputs(rng):
    return inputs(rng, 0, 0)
def setup_inputs_blocks(rng):
    return inputs(rng, 2, 0)
def setup_inputs_wide(rng):
    return inputs(rng, 0, 4)
def setup_inputs_faint(rng):
    d = setup_inputs(rng); d["gr"] = mx_ref.flush((d["gr"].astype(np.float32) * np.float32(2.0 ** -12)).astype(BF))
    return d
def reference(wc, ws, gr, x):
    S = [pick(t) for t in range(4)]
    H = [mx_ref.quantize(tile([mx_ref.matmul(S[t], pk(wc[j], ws[j], i)) - cut(gr[j], i).astype(np.float32)[:, t::4] * LR for t in range(4)])) for j in range(N) for i in range(WT)]
    y = np.zeros((N, 128, N * WT * NC), np.float32)
    for r in range(N):
        X = mx_ref.quantize(x[r])
        for b in range(N * WT):
            y[r][:, NC * b:NC * b + NC] = mx_ref.matmul(H[b], X)
    return {"y": y}

@@ -1,0 +1,126 @@
+from concourse.bass import DstId, RemoteDMATransfer
+from concourse.mybir import dt, AluOpType, ActivationFunctionType
+
+N, WT, NC = 3, 2, 128
+WC = WT * NC
+SPLIT = 640
+LR = 0.25
+
+SCRATCH = {
+    "wq": ("sbuf", [128, WC], "float8_e4m3fn_x4"),
+    "wp": ("sbuf", [128, WC], "uint8"),
+    "gt": ("sbuf", [128, 4 * WC], "bfloat16"),
+    "gs": ("sbuf", [128, 4 * WC], "bfloat16"),
+    "xt": ("sbuf", [128, 4 * NC], "bfloat16"),
+    "xq": ("sbuf", [128, NC], "float8_e4m3fn_x4"),
+    "xp": ("sbuf", [128, NC], "uint8"),
+    "z": ("sbuf", [128, 4 * NC + 4], "bfloat16"),
+    "sq": ("sbuf", [128, 4 * NC], "float8_e4m3fn_x4"),
+    "sp": ("sbuf", [128, 4 * NC], "uint8"),
+    "v": ("sbuf", [128, 4 * WC], "bfloat16"),
+    "vq": ("sbuf", [128, WC], "float8_e4m3fn_x4"),
+    "vp": ("sbuf", [128, WC], "uint8"),
+    "yb": ("sbuf", [128, N * WC], "float32"),
+    "pd": ("psum", [128, 512 * 4], "float32"),
+    "py": ("psum", [128, 512 * 4], "float32"),
+}
+for _j in range(N):
+    SCRATCH["lq%d" % _j] = ("sbuf", [128, WC], "float8_e4m3fn_x4")
+    SCRATCH["lp%d" % _j] = ("sbuf", [128, WC], "uint8")
+
+SEMAPHORES = (["wl", "gl", "xl", "zf", "zd", "gv", "ga", "sub", "vd", "xd", "sent", "st"]
+              + ["s%d" % b for b in range(4)] + ["d%d" % b for b in range(4)]
+              + ["arr%d" % j for j in range(N)]
+              + ["m%d" % k for k in range(N * WT)] + ["cv%d" % k for k in range(N)] + ["ca%d" % k for k in range(N)])
+
+
+def engines(mask, first, count):
+    bits = [e for e in range(16) if mask >> e & 1][first:first + count]
+    return sum(1 << e for e in bits)
+
+
+def dst_id(topo, c):
+    a = topo.addr(c)
+    return DstId(rid=a[0], pnc=a[1])
+
+
+def rank_program(g, core, T, topo):
+    rank = T.rank_of(core)
+    if rank is None:
+        return
+    s = T.sem
+    others = [j for j in range(N) if j != rank]
+    others.sort(key=lambda j: 0 if topo.same_plane(topo.chip(core), topo.chip(T.cores[j])) else 1)
+
+    g.sync.dma_start(T.wq[:, :].bitcast(dt.uint8), T.wc[:, :]).then_inc(s.wl, 16)
+    g.scalar.dma_start(T.wp[:, :], T.ws[:, :]).then_inc(s.wl, 16)
+    g.scalar.dma_start(T.gt[:, :], T.gr[:, :]).then_inc(s.gl, 16)
+    g.sync.dma_start(T.xt[:, :], T.x[:, :]).then_inc(s.xl, 16)
+
+    g.vector.memset(T.z[:, :], 0.0).then_inc(s.zf, 1)
+    g.wait_ge(s.zf, 1)
+    diag = T.z[:, 3:3 + 4 * NC:4]
+    g.affine_select(diag, diag, [[-1, NC]], AluOpType.not_equal, 1.0, 0, 1).then_inc(s.zd, 1)
+    g.vector.wait_ge(s.zd, 1)
+    for b in range(4):
+        g.vector.quantize_mx(T.sq[:, NC * b:NC * b + NC], T.sp[:, NC * b:NC * b + NC],
+                             T.z[:, 3 - b:3 - b + 4 * NC]).then_inc(s["s%d" % b], 1)
+
+    g.tensor.wait_ge(s.wl, 32)
+    for b in range(4):
+        g.tensor.wait_ge(s["s%d" % b], 1)
+        g.tensor.matmul_mx(T.pd[:, 512 * b:512 * b + WC], T.sq[:, NC * b:NC * b + NC], T.sp[:, NC * b:NC * b + NC],
+                           T.wq[:, :], T.wp[:, :], True, True).then_inc(s["d%d" % b], 1)
+
+    g.scalar.wait_ge(s.gl, 16)
+    g.scalar.activation(T.gs[:, SPLIT:4 * WC], T.gt[:, SPLIT:4 * WC], ActivationFunctionType.Copy, scale=LR).then_inc(s.ga, 1)
+    g.vector.wait_ge(s.gl, 16)
+    g.vector.tensor_scalar(T.gs[:, 0:SPLIT], T.gt[:, 0:SPLIT], LR, None, AluOpType.mult).then_inc(s.gv, 1)
+    g.vector.wait_ge(s.gv, 1)
+    g.vector.wait_ge(s.ga, 1)
+    for b in range(4):
+        g.vector.wait_ge(s["d%d" % b], 1)
+        g.vector.tensor_tensor(T.v[:, b:4 * WC:4], T.pd[:, 512 * b:512 * b + WC], T.gs[:, b:4 * WC:4],
+                               AluOpType.subtract).then_inc(s.sub, 1)
+    g.vector.wait_ge(s.sub, 4)
+    g.vector.quantize_mx(T.vq[:, :], T.vp[:, :], T.v[:, :]).then_inc(s.vd, 1)
+    g.vector.wait_ge(s.xl, 16)
+    g.vector.quantize_mx(T.xq[:, :], T.xp[:, :], T.xt[:, :]).then_inc(s.xd, 1)
+
+    m = topo.mask(core, T.cores[others[0]]) & topo.mask(core, T.cores[others[1]])
+    m = engines(m, 0, 8)
+    ids = [dst_id(topo, T.cores[j]) for j in others]
+    lq, lp = T["lq%d" % rank], T["lp%d" % rank]
+    g.wait_ge(s.vd, 1)
+    g.remote_dma_fused([RemoteDMATransfer(dst_ids=ids, dma_engine_mask=m, remote_sem=s["arr%d" % rank],
+                                          srcs=[T.vq[:, :].bitcast(dt.uint8)],
+                                          dsts=[lq[:, :].bitcast(dt.uint8) for j in others])], local_sem=s.sent)
+    g.remote_dma_fused([RemoteDMATransfer(dst_ids=ids, dma_engine_mask=m, remote_sem=s["arr%d" % rank],
+                                          srcs=[T.vp[:, :]], dsts=[lp[:, :] for j in others])], local_sem=s.sent)
+
+    banks = [(T.py, 0), (T.py, 1), (T.py, 2), (T.py, 3), (T.pd, 0), (T.pd, 1)]
+    g.tensor.wait_ge(s.vd, 1)
+    g.tensor.wait_ge(s.xd, 1)
+    for k, j in enumerate([rank] + others):
+        q, p = (T.vq, T.vp) if j == rank else (T["lq%d" % j], T["lp%d" % j])
+        if j != rank:
+            g.tensor.wait_ge(s["arr%d" % j], 16)
+        for i in range(WT):
+            n = WT * k + i
+            ps, bank = banks[n]
+            view = ps[:, 512 * bank:512 * bank + NC]
+            g.tensor.matmul_mx(view, q[:, NC * i:NC * i + NC], p[:, NC * i:NC * i + NC],
+                               T.xq[:, :], T.xp[:, :], True, True).then_inc(s["m%d" % n], 1)
+            out = T.yb[:, WC * j + NC * i:WC * j + NC * i + NC]
+            if i == 0:
+                g.vector.wait_ge(s["m%d" % n], 1)
+                g.vector.tensor_copy(out, view).then_inc(s["cv%d" % k], 1)
+            else:
+                g.scalar.wait_ge(s["m%d" % n], 1)
+                g.scalar.activation(out, view, ActivationFunctionType.Copy).then_inc(s["ca%d" % k], 1)
+        g.sync.wait_ge(s["cv%d" % k], 1)
+        g.sync.wait_ge(s["ca%d" % k], 1)
+        g.sync.dma_start(T.y[:, WC * j:WC * j + WC], T.yb[:, WC * j:WC * j + WC]).then_inc(s.st, 16)
+
+    g.sync.wait_ge(s.st, 16 * N)
+    g.wait_ge(s.sent, 16)

@@ -3,7 +3,7 @@ from concourse.mybir import dt, AluOpType, ActivationFunctionType
 
 N, WT, NC = 3, 2, 128
 WC = WT * NC
-SPLIT = 640
+TE = 4 * NC
 LR = 0.25
 
 SCRATCH = {
@@ -11,31 +11,32 @@ SCRATCH = {
     "wp": ("sbuf", [128, WC], "uint8"),
     "gt": ("sbuf", [128, 4 * WC], "bfloat16"),
     "gs": ("sbuf", [128, 4 * WC], "bfloat16"),
-    "xt": ("sbuf", [128, 4 * NC], "bfloat16"),
+    "xt": ("sbuf", [128, TE], "bfloat16"),
     "xq": ("sbuf", [128, NC], "float8_e4m3fn_x4"),
     "xp": ("sbuf", [128, NC], "uint8"),
-    "z": ("sbuf", [128, 4 * NC + 4], "bfloat16"),
+    "z": ("sbuf", [128, TE + 4], "bfloat16"),
     "sq": ("sbuf", [128, 4 * NC], "float8_e4m3fn_x4"),
     "sp": ("sbuf", [128, 4 * NC], "uint8"),
     "v": ("sbuf", [128, 4 * WC], "bfloat16"),
     "vq": ("sbuf", [128, WC], "float8_e4m3fn_x4"),
     "vp": ("sbuf", [128, WC], "uint8"),
     "yb": ("sbuf", [128, N * WC], "float32"),
-    "pd": ("psum", [128, 512 * 4], "float32"),
-    "py": ("psum", [128, 512 * 4], "float32"),
+    "pa": ("psum", [128, 512 * 4], "float32"),
+    "pb": ("psum", [128, 512 * 4], "float32"),
 }
 for _j in range(N):
     SCRATCH["lq%d" % _j] = ("sbuf", [128, WC], "float8_e4m3fn_x4")
     SCRATCH["lp%d" % _j] = ("sbuf", [128, WC], "uint8")
 
-SEMAPHORES = (["wl", "gl", "xl", "zf", "zd", "gv", "ga", "sub", "vd", "xd", "sent", "st"]
-              + ["s%d" % b for b in range(4)] + ["d%d" % b for b in range(4)]
-              + ["arr%d" % j for j in range(N)]
-              + ["m%d" % k for k in range(N * WT)] + ["cv%d" % k for k in range(N)] + ["ca%d" % k for k in range(N)])
+SEMAPHORES = (["wl0", "wl1", "pl", "gl0", "gl1", "xl", "zf", "zd", "gs0", "gs1", "sub0", "sub1", "vd0", "vd1", "xd",
+               "sent", "st"]
+              + ["s%d" % b for b in range(4)] + ["d%d" % b for b in range(4 * WT)]
+              + ["arr%d_%d" % (j, i) for j in range(N) for i in range(WT)]
+              + ["m%d" % k for k in range(N * WT)] + ["c%d" % k for k in range(N * WT)])
 
 
-def engines(mask, first, count):
-    bits = [e for e in range(16) if mask >> e & 1][first:first + count]
+def engines(mask, count):
+    bits = [e for e in range(16) if mask >> e & 1][:count]
     return sum(1 << e for e in bits)
 
 
@@ -52,75 +53,88 @@ def rank_program(g, core, T, topo):
     others = [j for j in range(N) if j != rank]
     others.sort(key=lambda j: 0 if topo.same_plane(topo.chip(core), topo.chip(T.cores[j])) else 1)
 
-    g.sync.dma_start(T.wq[:, :].bitcast(dt.uint8), T.wc[:, :]).then_inc(s.wl, 16)
-    g.scalar.dma_start(T.wp[:, :], T.ws[:, :]).then_inc(s.wl, 16)
-    g.scalar.dma_start(T.gt[:, :], T.gr[:, :]).then_inc(s.gl, 16)
+    g.sync.dma_start(T.wq[:, 0:NC].bitcast(dt.uint8), T.wc[:, 0:TE]).then_inc(s.wl0, 16)
+    g.scalar.dma_start(T.gt[:, 0:TE], T.gr[:, 0:TE]).then_inc(s.gl0, 16)
+    g.sync.dma_start(T.wp[:, :], T.ws[:, :]).then_inc(s.pl, 16)
+    g.scalar.dma_start(T.gt[:, TE:2 * TE], T.gr[:, TE:2 * TE]).then_inc(s.gl1, 16)
+    g.sync.dma_start(T.wq[:, NC:WC].bitcast(dt.uint8), T.wc[:, TE:2 * TE]).then_inc(s.wl1, 16)
     g.sync.dma_start(T.xt[:, :], T.x[:, :]).then_inc(s.xl, 16)
 
     g.vector.memset(T.z[:, :], 0.0).then_inc(s.zf, 1)
     g.wait_ge(s.zf, 1)
-    diag = T.z[:, 3:3 + 4 * NC:4]
+    diag = T.z[:, 3:3 + TE:4]
     g.affine_select(diag, diag, [[-1, NC]], AluOpType.not_equal, 1.0, 0, 1).then_inc(s.zd, 1)
     g.vector.wait_ge(s.zd, 1)
     for b in range(4):
         g.vector.quantize_mx(T.sq[:, NC * b:NC * b + NC], T.sp[:, NC * b:NC * b + NC],
-                             T.z[:, 3 - b:3 - b + 4 * NC]).then_inc(s["s%d" % b], 1)
+                             T.z[:, 3 - b:3 - b + TE]).then_inc(s["s%d" % b], 1)
 
-    g.tensor.wait_ge(s.wl, 32)
-    for b in range(4):
-        g.tensor.wait_ge(s["s%d" % b], 1)
-        g.tensor.matmul_mx(T.pd[:, 512 * b:512 * b + WC], T.sq[:, NC * b:NC * b + NC], T.sp[:, NC * b:NC * b + NC],
-                           T.wq[:, :], T.wp[:, :], True, True).then_inc(s["d%d" % b], 1)
+    g.tensor.wait_ge(s.pl, 16)
+    for i, pd in ((0, T.pa), (1, T.pb)):
+        g.tensor.wait_ge(s["wl%d" % i], 16)
+        for b in range(4):
+            if i == 0:
+                g.tensor.wait_ge(s["s%d" % b], 1)
+            g.tensor.matmul_mx(pd[:, 512 * b:512 * b + NC], T.sq[:, NC * b:NC * b + NC], T.sp[:, NC * b:NC * b + NC],
+                               T.wq[:, NC * i:NC * i + NC], T.wp[:, NC * i:NC * i + NC],
+                               True, True).then_inc(s["d%d" % (4 * i + b)], 1)
 
-    g.scalar.wait_ge(s.gl, 16)
-    g.scalar.activation(T.gs[:, SPLIT:4 * WC], T.gt[:, SPLIT:4 * WC], ActivationFunctionType.Copy, scale=LR).then_inc(s.ga, 1)
-    g.vector.wait_ge(s.gl, 16)
-    g.vector.tensor_scalar(T.gs[:, 0:SPLIT], T.gt[:, 0:SPLIT], LR, None, AluOpType.mult).then_inc(s.gv, 1)
-    g.vector.wait_ge(s.gv, 1)
-    g.vector.wait_ge(s.ga, 1)
-    for b in range(4):
-        g.vector.wait_ge(s["d%d" % b], 1)
-        g.vector.tensor_tensor(T.v[:, b:4 * WC:4], T.pd[:, 512 * b:512 * b + WC], T.gs[:, b:4 * WC:4],
-                               AluOpType.subtract).then_inc(s.sub, 1)
-    g.vector.wait_ge(s.sub, 4)
-    g.vector.quantize_mx(T.vq[:, :], T.vp[:, :], T.v[:, :]).then_inc(s.vd, 1)
+    g.scalar.wait_ge(s.gl1, 16)
+    g.scalar.activation(T.gs[:, TE:2 * TE], T.gt[:, TE:2 * TE], ActivationFunctionType.Copy, scale=LR).then_inc(s.gs1, 1)
+    g.vector.wait_ge(s.gl0, 16)
+    g.vector.tensor_scalar(T.gs[:, 0:TE], T.gt[:, 0:TE], LR, None, AluOpType.mult).then_inc(s.gs0, 1)
+    for i, pd in ((0, T.pa), (1, T.pb)):
+        g.vector.wait_ge(s["gs%d" % i], 1)
+        for b in range(4):
+            g.vector.wait_ge(s["d%d" % (4 * i + b)], 1)
+            g.vector.tensor_tensor(T.v[:, TE * i + b:TE * i + TE:4], pd[:, 512 * b:512 * b + NC],
+                                   T.gs[:, TE * i + b:TE * i + TE:4], AluOpType.subtract).then_inc(s["sub%d" % i], 1)
+        g.vector.wait_ge(s["sub%d" % i], 4)
+        g.vector.quantize_mx(T.vq[:, NC * i:NC * i + NC], T.vp[:, NC * i:NC * i + NC],
+                             T.v[:, TE * i:TE * i + TE]).then_inc(s["vd%d" % i], 1)
     g.vector.wait_ge(s.xl, 16)
     g.vector.quantize_mx(T.xq[:, :], T.xp[:, :], T.xt[:, :]).then_inc(s.xd, 1)
 
-    m = topo.mask(core, T.cores[others[0]]) & topo.mask(core, T.cores[others[1]])
-    m = engines(m, 0, 8)
+    ne = 8
+    m = engines(topo.mask(core, T.cores[others[0]]) & topo.mask(core, T.cores[others[1]]), ne)
     ids = [dst_id(topo, T.cores[j]) for j in others]
     lq, lp = T["lq%d" % rank], T["lp%d" % rank]
-    g.wait_ge(s.vd, 1)
-    g.remote_dma_fused([RemoteDMATransfer(dst_ids=ids, dma_engine_mask=m, remote_sem=s["arr%d" % rank],
-                                          srcs=[T.vq[:, :].bitcast(dt.uint8)],
-                                          dsts=[lq[:, :].bitcast(dt.uint8) for j in others])], local_sem=s.sent)
-    g.remote_dma_fused([RemoteDMATransfer(dst_ids=ids, dma_engine_mask=m, remote_sem=s["arr%d" % rank],
-                                          srcs=[T.vp[:, :]], dsts=[lp[:, :] for j in others])], local_sem=s.sent)
 
-    banks = [(T.py, 0), (T.py, 1), (T.py, 2), (T.py, 3), (T.pd, 0), (T.pd, 1)]
-    g.tensor.wait_ge(s.vd, 1)
+    def send(src, dst, i):
+        g.remote_dma_fused([RemoteDMATransfer(dst_ids=ids, dma_engine_mask=m, remote_sem=s["arr%d_%d" % (rank, i)],
+                                              srcs=[src], dsts=[dst for j in others])], local_sem=s.sent)
+    g.wait_ge(s.vd0, 1)
+    send(T.vq[:, 0:NC].bitcast(dt.uint8), lq[:, 0:NC].bitcast(dt.uint8), 0)
+    g.wait_ge(s.vd1, 1)
+    send(T.vp[:, :], lp[:, :], 0)
+    send(T.vq[:, NC:WC].bitcast(dt.uint8), lq[:, NC:WC].bitcast(dt.uint8), 1)
+
+    banks = [(T.pa, 0), (T.pa, 1), (T.pa, 2), (T.pa, 3), (T.pb, 0), (T.pb, 1)]
+    g.tensor.wait_ge(s.vd1, 1)
     g.tensor.wait_ge(s.xd, 1)
-    for k, j in enumerate([rank] + others):
+    stores = 0
+    for n, (j, i) in enumerate([(rank, 0), (rank, 1)] + [(j, i) for i in range(WT) for j in others]):
         q, p = (T.vq, T.vp) if j == rank else (T["lq%d" % j], T["lp%d" % j])
         if j != rank:
-            g.tensor.wait_ge(s["arr%d" % j], 16)
-        for i in range(WT):
-            n = WT * k + i
-            ps, bank = banks[n]
-            view = ps[:, 512 * bank:512 * bank + NC]
-            g.tensor.matmul_mx(view, q[:, NC * i:NC * i + NC], p[:, NC * i:NC * i + NC],
-                               T.xq[:, :], T.xp[:, :], True, True).then_inc(s["m%d" % n], 1)
-            out = T.yb[:, WC * j + NC * i:WC * j + NC * i + NC]
-            if i == 0:
-                g.vector.wait_ge(s["m%d" % n], 1)
-                g.vector.tensor_copy(out, view).then_inc(s["cv%d" % k], 1)
-            else:
-                g.scalar.wait_ge(s["m%d" % n], 1)
-                g.scalar.activation(out, view, ActivationFunctionType.Copy).then_inc(s["ca%d" % k], 1)
-        g.sync.wait_ge(s["cv%d" % k], 1)
-        g.sync.wait_ge(s["ca%d" % k], 1)
-        g.sync.dma_start(T.y[:, WC * j:WC * j + WC], T.yb[:, WC * j:WC * j + WC]).then_inc(s.st, 16)
+            g.tensor.wait_ge(s["arr%d_%d" % (j, i)], ne * (2 - i))
+        ps, bank = banks[n]
+        view = ps[:, 512 * bank:512 * bank + NC]
+        g.tensor.matmul_mx(view, q[:, NC * i:NC * i + NC], p[:, NC * i:NC * i + NC],
+                           T.xq[:, :], T.xp[:, :], True, True).then_inc(s["m%d" % n], 1)
+        at = WC * j + NC * i
+        out = T.yb[:, at:at + NC]
+        m_, c_ = s["m%d" % n], s["c%d" % n]
+        if n % 2 == 0:
+            g.vector.wait_ge(m_, 1)
+            g.vector.tensor_copy(out, view).then_inc(c_, 1)
+            g.sync.wait_ge(c_, 1)
+            g.sync.dma_start(T.y[:, at:at + NC], out).then_inc(s.st, 16)
+        else:
+            g.scalar.wait_ge(m_, 1)
+            g.scalar.activation(out, view, ActivationFunctionType.Copy).then_inc(c_, 1)
+            g.scalar.wait_ge(c_, 1)
+            g.scalar.dma_start(T.y[:, at:at + NC], out).then_inc(s.st, 16)
+        stores += 1
 
-    g.sync.wait_ge(s.st, 16 * N)
-    g.wait_ge(s.sent, 16)
+    g.sync.wait_ge(s.st, 16 * stores)
+    g.wait_ge(s.sent, 3 * ne)

@@ -14,6 +14,7 @@ SCRATCH = {
     "xt": ("sbuf", [128, TE], "bfloat16"),
     "xq": ("sbuf", [128, NC], "float8_e4m3fn_x4"),
     "xp": ("sbuf", [128, NC], "uint8"),
+    "ix": ("sbuf", [128, NC], "bfloat16"),
     "z": ("sbuf", [128, TE + 4], "bfloat16"),
     "sq": ("sbuf", [128, 4 * NC], "float8_e4m3fn_x4"),
     "sp": ("sbuf", [128, 4 * NC], "uint8"),
@@ -28,16 +29,25 @@ for _j in range(N):
     SCRATCH["lq%d" % _j] = ("sbuf", [128, WC], "float8_e4m3fn_x4")
     SCRATCH["lp%d" % _j] = ("sbuf", [128, WC], "uint8")
 
-SEMAPHORES = (["wl0", "wl1", "pl", "gl0", "gl1", "xl", "zf", "zd", "gs0", "gs1", "sub0", "sub1", "vd0", "vd1", "xd",
+SEMAPHORES = (["wl0", "wl1", "pl", "gl0", "gl1", "xl", "zf", "zi", "zd", "gv", "ga", "sub0", "sub1", "vd0", "vd1", "xd",
                "sent", "st"]
-              + ["s%d" % b for b in range(4)] + ["d%d" % b for b in range(4 * WT)]
+              + ["s%d" % b for b in range(4)] + ["h%d" % b for b in range(4)] + ["d%d" % b for b in range(4 * WT)]
               + ["arr%d_%d" % (j, i) for j in range(N) for i in range(WT)]
               + ["m%d" % k for k in range(N * WT)] + ["c%d" % k for k in range(N * WT)])
 
 
-def engines(mask, count):
-    bits = [e for e in range(16) if mask >> e & 1][:count]
+def engines(mask, first, step):
+    bits = [e for e in range(16) if mask >> e & 1][first::step]
     return sum(1 << e for e in bits)
+
+
+def count(mask):
+    return sum(mask >> e & 1 for e in range(16))
+
+
+def send_masks(T, topo, j):
+    m = topo.mask(T.cores[j], T.cores[(j + 1) % N]) & topo.mask(T.cores[j], T.cores[(j + 2) % N])
+    return m, {(j + 1) % N: engines(m, 0, 2), (j + 2) % N: engines(m, 1, 2)}
 
 
 def dst_id(topo, c):
@@ -50,20 +60,20 @@ def rank_program(g, core, T, topo):
     if rank is None:
         return
     s = T.sem
-    others = [j for j in range(N) if j != rank]
-    others.sort(key=lambda j: 0 if topo.same_plane(topo.chip(core), topo.chip(T.cores[j])) else 1)
+    nxt, prv = (rank + 1) % N, (rank + 2) % N
 
     g.sync.dma_start(T.wq[:, 0:NC].bitcast(dt.uint8), T.wc[:, 0:TE]).then_inc(s.wl0, 16)
-    g.scalar.dma_start(T.gt[:, 0:TE], T.gr[:, 0:TE]).then_inc(s.gl0, 16)
-    g.sync.dma_start(T.wp[:, :], T.ws[:, :]).then_inc(s.pl, 16)
-    g.scalar.dma_start(T.gt[:, TE:2 * TE], T.gr[:, TE:2 * TE]).then_inc(s.gl1, 16)
+    g.scalar.dma_start(T.wp[:, :], T.ws[:, :]).then_inc(s.pl, 16)
+    g.sync.dma_start(T.gt[:, 0:TE], T.gr[:, 0:TE]).then_inc(s.gl0, 16)
     g.sync.dma_start(T.wq[:, NC:WC].bitcast(dt.uint8), T.wc[:, TE:2 * TE]).then_inc(s.wl1, 16)
+    g.sync.dma_start(T.gt[:, TE:2 * TE], T.gr[:, TE:2 * TE]).then_inc(s.gl1, 16)
     g.sync.dma_start(T.xt[:, :], T.x[:, :]).then_inc(s.xl, 16)
 
+    g.iota(T.ix[:, :], [[-1, NC]], 0, 1, allow_small_or_imprecise_dtypes=True).then_inc(s.zi, 1)
     g.vector.memset(T.z[:, :], 0.0).then_inc(s.zf, 1)
-    g.wait_ge(s.zf, 1)
-    diag = T.z[:, 3:3 + TE:4]
-    g.affine_select(diag, diag, [[-1, NC]], AluOpType.not_equal, 1.0, 0, 1).then_inc(s.zd, 1)
+    g.vector.wait_ge(s.zf, 1)
+    g.vector.wait_ge(s.zi, 1)
+    g.vector.tensor_scalar(T.z[:, 3:3 + TE:4], T.ix[:, :], 0.0, None, AluOpType.is_equal).then_inc(s.zd, 1)
     g.vector.wait_ge(s.zd, 1)
     for b in range(4):
         g.vector.quantize_mx(T.sq[:, NC * b:NC * b + NC], T.sp[:, NC * b:NC * b + NC],
@@ -79,13 +89,22 @@ def rank_program(g, core, T, topo):
                                T.wq[:, NC * i:NC * i + NC], T.wp[:, NC * i:NC * i + NC],
                                True, True).then_inc(s["d%d" % (4 * i + b)], 1)
 
-    g.scalar.wait_ge(s.gl1, 16)
-    g.scalar.activation(T.gs[:, TE:2 * TE], T.gt[:, TE:2 * TE], ActivationFunctionType.Copy, scale=LR).then_inc(s.gs1, 1)
     g.vector.wait_ge(s.gl0, 16)
-    g.vector.tensor_scalar(T.gs[:, 0:TE], T.gt[:, 0:TE], LR, None, AluOpType.mult).then_inc(s.gs0, 1)
+    g.scalar.wait_ge(s.gl0, 16)
+    for b in range(2):
+        g.vector.tensor_scalar(T.gs[:, b:TE:4], T.gt[:, b:TE:4], LR, None, AluOpType.mult).then_inc(s.gv, 1)
+        g.scalar.activation(T.gs[:, b + 2:TE:4], T.gt[:, b + 2:TE:4], ActivationFunctionType.Copy, scale=LR).then_inc(s.ga, 1)
+    g.scalar.wait_ge(s.gl1, 16)
+    for b in range(4):
+        g.scalar.activation(T.gs[:, TE + b:2 * TE:4], T.gt[:, TE + b:2 * TE:4], ActivationFunctionType.Copy,
+                            scale=LR).then_inc(s["h%d" % b], 1)
+
     for i, pd in ((0, T.pa), (1, T.pb)):
-        g.vector.wait_ge(s["gs%d" % i], 1)
         for b in range(4):
+            if i == 1:
+                g.vector.wait_ge(s["h%d" % b], 1)
+            elif b % 2 == 0:
+                g.vector.wait_ge(s.ga if b else s.gv, 2)
             g.vector.wait_ge(s["d%d" % (4 * i + b)], 1)
             g.vector.tensor_tensor(T.v[:, TE * i + b:TE * i + TE:4], pd[:, 512 * b:512 * b + NC],
                                    T.gs[:, TE * i + b:TE * i + TE:4], AluOpType.subtract).then_inc(s["sub%d" % i], 1)
@@ -95,28 +114,30 @@ def rank_program(g, core, T, topo):
     g.vector.wait_ge(s.xl, 16)
     g.vector.quantize_mx(T.xq[:, :], T.xp[:, :], T.xt[:, :]).then_inc(s.xd, 1)
 
-    ne = 8
-    m = engines(topo.mask(core, T.cores[others[0]]) & topo.mask(core, T.cores[others[1]]), ne)
-    ids = [dst_id(topo, T.cores[j]) for j in others]
+    m, half = send_masks(T, topo, rank)
     lq, lp = T["lq%d" % rank], T["lp%d" % rank]
 
-    def send(src, dst, i):
-        g.remote_dma_fused([RemoteDMATransfer(dst_ids=ids, dma_engine_mask=m, remote_sem=s["arr%d_%d" % (rank, i)],
-                                              srcs=[src], dsts=[dst for j in others])], local_sem=s.sent)
+    def send(src, dst, i, to, mask):
+        g.remote_dma_fused([RemoteDMATransfer(dst_ids=[dst_id(topo, T.cores[j]) for j in to], dma_engine_mask=mask,
+                                              remote_sem=s["arr%d_%d" % (rank, i)],
+                                              srcs=[src], dsts=[dst for j in to])], local_sem=s.sent)
     g.wait_ge(s.vd0, 1)
-    send(T.vq[:, 0:NC].bitcast(dt.uint8), lq[:, 0:NC].bitcast(dt.uint8), 0)
+    for j in (nxt, prv):
+        send(T.vq[:, 0:NC].bitcast(dt.uint8), lq[:, 0:NC].bitcast(dt.uint8), 0, [j], half[j])
     g.wait_ge(s.vd1, 1)
-    send(T.vp[:, :], lp[:, :], 0)
-    send(T.vq[:, NC:WC].bitcast(dt.uint8), lq[:, NC:WC].bitcast(dt.uint8), 1)
+    send(T.vp[:, :], lp[:, :], 0, [nxt, prv], m)
+    for j in (nxt, prv):
+        send(T.vq[:, NC:WC].bitcast(dt.uint8), lq[:, NC:WC].bitcast(dt.uint8), 1, [j], m)
 
     banks = [(T.pa, 0), (T.pa, 1), (T.pa, 2), (T.pa, 3), (T.pb, 0), (T.pb, 1)]
     g.tensor.wait_ge(s.vd1, 1)
     g.tensor.wait_ge(s.xd, 1)
     stores = 0
-    for n, (j, i) in enumerate([(rank, 0), (rank, 1)] + [(j, i) for i in range(WT) for j in others]):
+    for n, (j, i) in enumerate([(rank, 0), (rank, 1)] + [(j, i) for i in range(WT) for j in (prv, nxt)]):
         q, p = (T.vq, T.vp) if j == rank else (T["lq%d" % j], T["lp%d" % j])
         if j != rank:
-            g.tensor.wait_ge(s["arr%d_%d" % (j, i)], ne * (2 - i))
+            mj, hj = send_masks(T, topo, j)
+            g.tensor.wait_ge(s["arr%d_%d" % (j, i)], count(mj) + (0 if i else count(hj[rank])))
         ps, bank = banks[n]
         view = ps[:, 512 * bank:512 * bank + NC]
         g.tensor.matmul_mx(view, q[:, NC * i:NC * i + NC], p[:, NC * i:NC * i + NC],
@@ -137,4 +158,4 @@ def rank_program(g, core, T, topo):
         stores += 1
 
     g.sync.wait_ge(s.st, 16 * stores)
-    g.wait_ge(s.sent, 3 * ne)
+    g.wait_ge(s.sent, 3 * count(m) + sum(count(k) for k in half.values()))

from concourse.bass import DstId, RemoteDMATransfer
from concourse.mybir import dt, AluOpType, ActivationFunctionType

N, WT, NC = 3, 2, 128
WC = WT * NC
TE = 4 * NC
LR = 0.25

SCRATCH = {
    "wq": ("sbuf", [128, WC], "float8_e4m3fn_x4"),
    "wp": ("sbuf", [128, WC], "uint8"),
    "gt": ("sbuf", [128, 4 * WC], "bfloat16"),
    "gs": ("sbuf", [128, 4 * WC], "bfloat16"),
    "xt": ("sbuf", [128, TE], "bfloat16"),
    "xq": ("sbuf", [128, NC], "float8_e4m3fn_x4"),
    "xp": ("sbuf", [128, NC], "uint8"),
    "ix": ("sbuf", [128, NC], "bfloat16"),
    "z": ("sbuf", [128, TE + 4], "bfloat16"),
    "sq": ("sbuf", [128, 4 * NC], "float8_e4m3fn_x4"),
    "sp": ("sbuf", [128, 4 * NC], "uint8"),
    "v": ("sbuf", [128, 4 * WC], "bfloat16"),
    "vq": ("sbuf", [128, WC], "float8_e4m3fn_x4"),
    "vp": ("sbuf", [128, WC], "uint8"),
    "yb": ("sbuf", [128, N * WC], "float32"),
    "pa": ("psum", [128, 512 * 4], "float32"),
    "pb": ("psum", [128, 512 * 4], "float32"),
}
for _j in range(N):
    SCRATCH["lq%d" % _j] = ("sbuf", [128, WC], "float8_e4m3fn_x4")
    SCRATCH["lp%d" % _j] = ("sbuf", [128, WC], "uint8")

SEMAPHORES = (["wl0", "wl1", "pl", "gl0", "gl1", "xl", "zf", "zi", "zd", "gv", "ga", "sub0", "sub1", "vd0", "vd1", "xd",
               "sent", "st"]
              + ["s%d" % b for b in range(4)] + ["h%d" % b for b in range(4)] + ["d%d" % b for b in range(4 * WT)]
              + ["arr%d_%d" % (j, i) for j in range(N) for i in range(WT)]
              + ["m%d" % k for k in range(N * WT)] + ["c%d" % k for k in range(N * WT)])


def engines(mask, first, step):
    bits = [e for e in range(16) if mask >> e & 1][first::step]
    return sum(1 << e for e in bits)


def count(mask):
    return sum(mask >> e & 1 for e in range(16))


def send_masks(T, topo, j):
    m = topo.mask(T.cores[j], T.cores[(j + 1) % N]) & topo.mask(T.cores[j], T.cores[(j + 2) % N])
    return m, {(j + 1) % N: engines(m, 0, 2), (j + 2) % N: engines(m, 1, 2)}


def dst_id(topo, c):
    a = topo.addr(c)
    return DstId(rid=a[0], pnc=a[1])


def rank_program(g, core, T, topo):
    rank = T.rank_of(core)
    if rank is None:
        return
    s = T.sem
    nxt, prv = (rank + 1) % N, (rank + 2) % N

    g.sync.dma_start(T.wq[:, 0:NC].bitcast(dt.uint8), T.wc[:, 0:TE]).then_inc(s.wl0, 16)
    g.scalar.dma_start(T.wp[:, :], T.ws[:, :]).then_inc(s.pl, 16)
    g.sync.dma_start(T.gt[:, 0:TE], T.gr[:, 0:TE]).then_inc(s.gl0, 16)
    g.sync.dma_start(T.wq[:, NC:WC].bitcast(dt.uint8), T.wc[:, TE:2 * TE]).then_inc(s.wl1, 16)
    g.sync.dma_start(T.gt[:, TE:2 * TE], T.gr[:, TE:2 * TE]).then_inc(s.gl1, 16)
    g.sync.dma_start(T.xt[:, :], T.x[:, :]).then_inc(s.xl, 16)

    g.iota(T.ix[:, :], [[-1, NC]], 0, 1, allow_small_or_imprecise_dtypes=True).then_inc(s.zi, 1)
    g.vector.memset(T.z[:, :], 0.0).then_inc(s.zf, 1)
    g.vector.wait_ge(s.zf, 1)
    g.vector.wait_ge(s.zi, 1)
    g.vector.tensor_scalar(T.z[:, 3:3 + TE:4], T.ix[:, :], 0.0, None, AluOpType.is_equal).then_inc(s.zd, 1)
    g.vector.wait_ge(s.zd, 1)
    for b in range(4):
        g.vector.quantize_mx(T.sq[:, NC * b:NC * b + NC], T.sp[:, NC * b:NC * b + NC],
                             T.z[:, 3 - b:3 - b + TE]).then_inc(s["s%d" % b], 1)

    g.tensor.wait_ge(s.pl, 16)
    for i, pd in ((0, T.pa), (1, T.pb)):
        g.tensor.wait_ge(s["wl%d" % i], 16)
        for b in range(4):
            if i == 0:
                g.tensor.wait_ge(s["s%d" % b], 1)
            g.tensor.matmul_mx(pd[:, 512 * b:512 * b + NC], T.sq[:, NC * b:NC * b + NC], T.sp[:, NC * b:NC * b + NC],
                               T.wq[:, NC * i:NC * i + NC], T.wp[:, NC * i:NC * i + NC],
                               True, True).then_inc(s["d%d" % (4 * i + b)], 1)

    g.vector.wait_ge(s.gl0, 16)
    g.scalar.wait_ge(s.gl0, 16)
    for b in range(2):
        g.vector.tensor_scalar(T.gs[:, b:TE:4], T.gt[:, b:TE:4], LR, None, AluOpType.mult).then_inc(s.gv, 1)
        g.scalar.activation(T.gs[:, b + 2:TE:4], T.gt[:, b + 2:TE:4], ActivationFunctionType.Copy, scale=LR).then_inc(s.ga, 1)
    g.scalar.wait_ge(s.gl1, 16)
    for b in range(4):
        g.scalar.activation(T.gs[:, TE + b:2 * TE:4], T.gt[:, TE + b:2 * TE:4], ActivationFunctionType.Copy,
                            scale=LR).then_inc(s["h%d" % b], 1)

    for i, pd in ((0, T.pa), (1, T.pb)):
        for b in range(4):
            if i == 1:
                g.vector.wait_ge(s["h%d" % b], 1)
            elif b % 2 == 0:
                g.vector.wait_ge(s.ga if b else s.gv, 2)
            g.vector.wait_ge(s["d%d" % (4 * i + b)], 1)
            g.vector.tensor_tensor(T.v[:, TE * i + b:TE * i + TE:4], pd[:, 512 * b:512 * b + NC],
                                   T.gs[:, TE * i + b:TE * i + TE:4], AluOpType.subtract).then_inc(s["sub%d" % i], 1)
        g.vector.wait_ge(s["sub%d" % i], 4)
        g.vector.quantize_mx(T.vq[:, NC * i:NC * i + NC], T.vp[:, NC * i:NC * i + NC],
                             T.v[:, TE * i:TE * i + TE]).then_inc(s["vd%d" % i], 1)
    g.vector.wait_ge(s.xl, 16)
    g.vector.quantize_mx(T.xq[:, :], T.xp[:, :], T.xt[:, :]).then_inc(s.xd, 1)

    m, half = send_masks(T, topo, rank)
    lq, lp = T["lq%d" % rank], T["lp%d" % rank]

    def send(src, dst, i, to, mask):
        g.remote_dma_fused([RemoteDMATransfer(dst_ids=[dst_id(topo, T.cores[j]) for j in to], dma_engine_mask=mask,
                                              remote_sem=s["arr%d_%d" % (rank, i)],
                                              srcs=[src], dsts=[dst for j in to])], local_sem=s.sent)
    g.wait_ge(s.vd0, 1)
    for j in (nxt, prv):
        send(T.vq[:, 0:NC].bitcast(dt.uint8), lq[:, 0:NC].bitcast(dt.uint8), 0, [j], half[j])
    g.wait_ge(s.vd1, 1)
    send(T.vp[:, :], lp[:, :], 0, [nxt, prv], m)
    for j in (nxt, prv):
        send(T.vq[:, NC:WC].bitcast(dt.uint8), lq[:, NC:WC].bitcast(dt.uint8), 1, [j], m)

    banks = [(T.pa, 0), (T.pa, 1), (T.pa, 2), (T.pa, 3), (T.pb, 0), (T.pb, 1)]
    g.tensor.wait_ge(s.vd1, 1)
    g.tensor.wait_ge(s.xd, 1)
    stores = 0
    for n, (j, i) in enumerate([(rank, 0), (rank, 1)] + [(j, i) for i in range(WT) for j in (prv, nxt)]):
        q, p = (T.vq, T.vp) if j == rank else (T["lq%d" % j], T["lp%d" % j])
        if j != rank:
            mj, hj = send_masks(T, topo, j)
            g.tensor.wait_ge(s["arr%d_%d" % (j, i)], count(mj) + (0 if i else count(hj[rank])))
        ps, bank = banks[n]
        view = ps[:, 512 * bank:512 * bank + NC]
        g.tensor.matmul_mx(view, q[:, NC * i:NC * i + NC], p[:, NC * i:NC * i + NC],
                           T.xq[:, :], T.xp[:, :], True, True).then_inc(s["m%d" % n], 1)
        at = WC * j + NC * i
        out = T.yb[:, at:at + NC]
        m_, c_ = s["m%d" % n], s["c%d" % n]
        if n % 2 == 0:
            g.vector.wait_ge(m_, 1)
            g.vector.tensor_copy(out, view).then_inc(c_, 1)
            g.sync.wait_ge(c_, 1)
            g.sync.dma_start(T.y[:, at:at + NC], out).then_inc(s.st, 16)
        else:
            g.scalar.wait_ge(m_, 1)
            g.scalar.activation(out, view, ActivationFunctionType.Copy).then_inc(c_, 1)
            g.scalar.wait_ge(c_, 1)
            g.scalar.dma_start(T.y[:, at:at + NC], out).then_inc(s.st, 16)
        stores += 1

    g.sync.wait_ge(s.st, 16 * stores)
    g.wait_ge(s.sent, 3 * count(m) + sum(count(k) for k in half.values()))
